import numpy as np
import ml_dtypes


def mxq(x, axis, fmt="e4m3"):
    dtype, down = {"e4m3": (ml_dtypes.float8_e4m3fn, 7), "e5m2": (ml_dtypes.float8_e5m2, 14)}[fmt]
    v = np.moveaxis(np.asarray(x, np.float32).astype(ml_dtypes.bfloat16).astype(np.float64), axis, -1)
    blocks = v.reshape(v.shape[:-1] + (-1, 32))
    amax = np.abs(blocks).max(-1, keepdims=True)
    byte = np.maximum(np.where(amax > 0, np.frexp(amax)[1] - 1 + 127, 0) - down, 1)
    scale = np.exp2(byte - 127.0)
    codes = (blocks / scale).astype(np.float32).astype(dtype).astype(np.float64)
    return np.moveaxis((codes * scale).reshape(v.shape), -1, axis)


WIDE = False


def mx_kscale(k):
    if not WIDE:
        return np.ones(k)
    levels = np.array([10, -10, 5, -5, 0])
    if k % 512:
        return np.exp2(np.random.permutation(np.resize(levels, k // 32))).repeat(32)
    a = np.empty((k // 512, 16))
    for p in range(k // 512):
        a[p, :8] = np.random.permutation(np.resize(levels, 8))
        for g in range(8):
            far = levels[np.abs(levels - a[p, g]) >= 10]
            a[p, g + 8] = far[np.random.randint(len(far))]
    return np.exp2(a.ravel()).repeat(32)


def f64(x):
    return np.asarray(x).astype(np.float64)


def striped(idx):
    return np.tile(idx.reshape(-1, 16).T, (8, 1)).astype(np.uint16)


def unstriped(offs):
    return offs[:16].T.reshape(-1).astype(np.int64)


def striped8(idx):
    return np.concatenate([x.reshape(-1, 16).T for x in idx]).astype(np.uint16)


def runs(offs, k):
    lists = np.stack([offs[16 * r : 16 * r + 16].T.reshape(-1) for r in range(8)]).astype(np.int64)
    return lists[np.arange(k) % 512 // 64]


def pack_weight(w):
    k, n = w.shape
    w = f64(np.asarray(w, np.float32).astype(ml_dtypes.bfloat16)).reshape(k // 32, 32, n)
    amax = np.abs(w).max(1)
    byte = np.clip(np.where(amax > 0, np.frexp(amax)[1] - 1 + 127 - 7, 1), 1, 254)
    scaled = (w * np.exp2(127.0 - byte)[:, None, :]).reshape(k, n).astype(np.float32)
    words = np.ascontiguousarray(scaled.reshape(k // 512, 128, 4, n).transpose(0, 1, 3, 2)).astype(ml_dtypes.float8_e4m3fn).view(np.uint8)
    return words, np.ascontiguousarray(byte.astype(np.uint8).reshape(k // 512, 16, n))


def unpack_weight(words, scales):
    g, p, n, _ = words.shape
    vals = np.ascontiguousarray(words).view(ml_dtypes.float8_e4m3fn).astype(np.float64) * np.repeat(np.exp2(scales.astype(np.float64) - 127.0), 8, axis=1)[..., None]
    return vals.transpose(0, 1, 3, 2).reshape(g * 512, n)


def sigmoid(v):
    return 1.0 / (1.0 + np.exp(-np.maximum(v, -700.0)))


K, T, S, N, H, U = 512, 2048, 512, 512, 512, 1024


def setup_inputs():
    n = np.random.standard_normal
    s = mx_kscale(K)[:, None]
    u = mx_kscale(H)
    packed_xT = pack_weight(n((K, T)) * s)
    return {
        "x_words": packed_xT[0],
        "x_scales": packed_xT[1],
        "w1": (n((K, H)) / np.sqrt(K) / s).astype(np.float32),
        "mem": n((H, U)).astype(np.float32),
        "gn": (np.random.uniform(0.5, 1.5, (H, 1)) * u[:, None]).astype(np.float32),
        "w2": (n((H, N)) / np.sqrt(H) / u[:, None]).astype(np.float32),
        "offs": striped(np.random.permutation(T)[:S]),
        "slot": striped8(np.stack([np.random.permutation(U)[:S] for _ in range(8)])),
        "mate": striped8(np.stack([np.random.permutation(U) for _ in range(8)])),
    }


def reference(x_words, x_scales, w1, mem, gn, w2, offs, slot, mate):
    xq = unpack_weight(x_words, x_scales)[:, unstriped(offs)]
    y = mxq(f64(w1), 0, "e4m3").T @ xq
    nw = sigmoid(y) * (y - (f64(mem)[np.arange(H)[:, None], runs(slot, H)]))
    pg = f64(mem).copy()
    pg[np.arange(H)[:, None], runs(slot, H)] = nw
    z = f64(gn) * pg
    h = mxq(f64(w2), 0, "e4m3").T @ mxq(z, 0, "e4m3")
    return np.minimum(h, h[np.arange(N)[:, None], runs(mate, N)])

@@ -1,0 +1,162 @@
+from contextlib import ExitStack
+
+import concourse.mybir as mybir
+
+K, T, S, N, H, U = 512, 2048, 512, 512, 512, 1024
+FLOPS = 2 * K * H * S + 2 * H * N * U
+
+F32 = mybir.dt.float32
+BF16 = mybir.dt.bfloat16
+I32 = mybir.dt.int32
+U32 = mybir.dt.uint32
+U16 = mybir.dt.uint16
+U8 = mybir.dt.uint8
+FP8X4 = mybir.dt.float8_e4m3fn_x4
+ALU = mybir.AluOpType
+ACT = mybir.ActivationFunctionType
+
+P = 128
+PACK = 4
+HALF = U // 2
+QUARTER = U // 4
+PLANE_ORDER = (2, 0, 1, 3)
+
+
+def tile_picked_pagemin_none_p_kernel(tc, x_words, x_scales, w1, mem, gn, w2, offs, slot, mate, out):
+    nc = tc.nc
+    with ExitStack() as ctx:
+        keep = ctx.enter_context(tc.tile_pool(name="keep", bufs=1))
+        ring = ctx.enter_context(tc.tile_pool(name="ring", bufs=2))
+        psum = ctx.enter_context(tc.psum_pool(name="psum", bufs=1))
+
+        offs_sb = keep.tile([P, S // 16], U16, name="offs_sb")
+        slot_sb = keep.tile([P, S // 16], U16, name="slot_sb")
+        mate_sb = keep.tile([P, U // 16], U16, name="mate_sb")
+        table_words = keep.tile([P, T], I32, name="table_words", align_bytes=64)
+        table_scales = keep.tile([P, T], U8, name="table_scales", align_bytes=64)
+        gain = keep.tile([P, PACK], F32, name="gain")
+        warm = keep.tile([P, 1], F32, name="warm")
+        warm2 = keep.tile([P, 1], F32, name="warm2")
+        w1_raw = [keep.tile([P, PACK, H // 2], F32, name="w1_raw%d" % c) for c in range(2)]
+        w2_raw = keep.tile([P, PACK, N], F32, name="w2_raw")
+        page = [keep.tile([P, U], F32, name="page%d" % t) for t in range(PACK)]
+
+        nc.vector.memset(table_scales[:].bitcast(I32), 0)
+        nc.vector.memset(warm[:], 0.0)
+        nc.sync.dma_start(offs_sb[:], offs)
+        for q in range(4):
+            nc.scalar.dma_start(table_scales[32 * q : 32 * q + 4, :].bitcast(I32), x_scales[0, 4 * q : 4 * q + 4, :].bitcast(I32))
+        nc.scalar.activation(warm2[:], warm[:], ACT.Sigmoid)
+        w1_rows = w1.rearrange("(p j) c -> p j c", j=PACK)
+        for c in range(2):
+            nc.sync.dma_start(w1_raw[c][:], w1_rows[:, :, c * (H // 2) : (c + 1) * (H // 2)])
+        nc.sync.dma_start(table_words[:], x_words[0].rearrange("p c r -> p (c r)").bitcast(I32))
+        nc.sync.dma_start(slot_sb[:], slot)
+        nc.sync.dma_start(gain[:], gn.rearrange("(p t) o -> p (t o)", t=PACK))
+        mem_rows = mem.rearrange("(p t) w -> t p w", t=PACK)
+        for t in PLANE_ORDER:
+            nc.sync.dma_start(page[t][:], mem_rows[t])
+        nc.sync.dma_start(w2_raw[:], w2.rearrange("(p j) c -> p j c", j=PACK))
+        nc.sync.dma_start(mate_sb[:], mate)
+
+        x_codes = keep.tile([P, S], U32, name="x_codes", align_bytes=64)
+        x_bytes = keep.tile([P, S], U8, name="x_bytes", align_bytes=64)
+        nc.vector.tensor_copy(x_bytes[:], table_scales[:].indirect(offs_sb[:]))
+
+        w1_bf = keep.tile([P, PACK * H], BF16, name="w1_bf", align_bytes=64)
+        w1_view = w1_bf[:].rearrange("p (t m j) -> p m j t", t=PACK, j=PACK)
+        src = [w1_raw[c][:].rearrange("p j (m t) -> p m j t", t=PACK) for c in range(2)]
+        nc.scalar.copy(w1_view[:, 0:64], src[0])
+        nc.vector.tensor_copy(w1_view[:, 64:128], src[1])
+        w1_codes = keep.tile([P, H], U32, name="w1_codes", align_bytes=64)
+        w1_scales = keep.tile([P, H], U8, name="w1_scales", align_bytes=64)
+        nc.vector.quantize_mx(out=w1_codes[:].bitcast(FP8X4), scales=w1_scales[:], in_=w1_bf[:])
+        nc.vector.tensor_copy(x_codes[:], table_words[:].bitcast(U32).indirect(offs_sb[:]))
+        y = {}
+        for t in PLANE_ORDER:
+            cols = slice(t * P, (t + 1) * P)
+            y[t] = psum.tile([P, S], F32, name="y", tag="bank%d" % t)
+            nc.tensor.matmul_mx(out=y[t][:], lhsT=w1_codes[:, cols].bitcast(FP8X4), lhsT_scale=w1_scales[:, cols],
+                                rhs=x_codes[:].bitcast(FP8X4), rhs_scale=x_bytes[:], start=True, stop=True)
+
+        z_bf = keep.tile([P, U * PACK], BF16, name="z_bf", align_bytes=64)
+        z_view = z_bf[:].rearrange("p (w t) -> p t w", t=PACK)
+        w2_bf = keep.tile([P, PACK * N], BF16, name="w2_bf", align_bytes=64)
+        w2_view = w2_bf[:].rearrange("p (t m j) -> p m j t", t=PACK, j=PACK)
+        w2_src = w2_raw[:].rearrange("p j (m t) -> p m j t", t=PACK)
+        w2_codes = keep.tile([P, N], U32, name="w2_codes", align_bytes=64)
+        w2_scales = keep.tile([P, N], U8, name="w2_scales", align_bytes=64)
+
+        diffs = {}
+        gates = {}
+
+        def fetch(t):
+            old = ring.tile([P, S], F32, name="old")
+            nc.vector.tensor_copy(old[:], page[t][:].indirect(slot_sb[:]))
+            gates[t] = ring.tile([P, S], F32, name="gate")
+            nc.scalar.activation(gates[t][:], y[t][:], ACT.Sigmoid)
+            if t == PLANE_ORDER[-1]:
+                diffs[t] = keep.tile([P, S], F32, name="last_diff", tag="page%d" % PLANE_ORDER[0])
+            else:
+                diffs[t] = ring.tile([P, S], F32, name="diff")
+            nc.vector.tensor_tensor(diffs[t][:], y[t][:], old[:], ALU.subtract)
+
+        def scale_plane(engine_is_vector, t, c0, c1):
+            if engine_is_vector:
+                nc.vector.tensor_scalar(z_view[:, t, c0:c1], page[t][:, c0:c1], gain[:, t : t + 1], None, ALU.mult)
+            else:
+                nc.scalar.activation(z_view[:, t, c0:c1], page[t][:, c0:c1], ACT.Copy, scale=gain[:, t : t + 1])
+
+        fetch(PLANE_ORDER[0])
+        for i, t in enumerate(PLANE_ORDER):
+            if i + 1 < PACK:
+                fetch(PLANE_ORDER[i + 1])
+            nc.vector.tensor_tensor(page[t][:].indirect(slot_sb[:]), diffs[t][:], gates[t][:], ALU.mult)
+            if i == 2:
+                nc.scalar.copy(w2_view[:, :, :, 0:2], w2_src[:, :, :, 0:2])
+                nc.vector.quantize_mx(out=w2_codes[:, 0 : 2 * P].bitcast(FP8X4), scales=w2_scales[:, 0 : 2 * P], in_=w2_bf[:, 0 : 2 * N])
+            if i + 1 < PACK:
+                scale_plane(False, t, 0, U)
+
+        last = PLANE_ORDER[-1]
+        z_codes = keep.tile([P, U], U32, name="z_codes", align_bytes=64)
+        z_scales = keep.tile([P, U], U8, name="z_scales", align_bytes=64)
+        scale_plane(False, last, HALF, HALF + QUARTER)
+        scale_plane(True, last, 0, HALF)
+        scale_plane(False, last, HALF + QUARTER, U)
+        pieces = ((HALF, HALF + QUARTER), (0, HALF), (HALF + QUARTER, U))
+        for c0, c1 in pieces:
+            nc.vector.quantize_mx(out=z_codes[:, c0:c1].bitcast(FP8X4), scales=z_scales[:, c0:c1], in_=z_bf[:, PACK * c0 : PACK * c1])
+        nc.vector.tensor_copy(w2_view[:, :, :, 2:4], w2_src[:, :, :, 2:4])
+
+        out_rows = out.rearrange("(p t) w -> t p w", t=PACK)
+        h = [keep.tile([P, U], F32, name="h%d" % t) for t in range(PACK)]
+        bank = [4]
+
+        def product(t, c0, c1):
+            cols = slice(t * P, (t + 1) * P)
+            acc = psum.tile([P, c1 - c0], F32, name="acc", tag="bank%d" % (bank[0] % 8))
+            bank[0] = bank[0] + 1
+            nc.tensor.matmul_mx(out=acc[:], lhsT=w2_codes[:, cols].bitcast(FP8X4), lhsT_scale=w2_scales[:, cols],
+                                rhs=z_codes[:, c0:c1].bitcast(FP8X4), rhs_scale=z_scales[:, c0:c1], start=True, stop=True)
+            nc.scalar.copy(h[t][:, c0:c1], acc[:])
+
+        for c0, c1 in pieces:
+            product(0, c0, c1)
+        nc.vector.quantize_mx(out=w2_codes[:, 2 * P : 4 * P].bitcast(FP8X4), scales=w2_scales[:, 2 * P : 4 * P], in_=w2_bf[:, 2 * N : 4 * N])
+        for t in range(1, PACK):
+            for c0 in (0, HALF):
+                product(t, c0, c0 + HALF)
+
+        steps = [(t, c0, c0 + HALF) for t in range(PACK) for c0 in (0, HALF)][:-1]
+        steps = steps + [(PACK - 1, HALF, HALF + QUARTER), (PACK - 1, HALF + QUARTER, U)]
+        mates = []
+        for i in range(len(steps) + 1):
+            if i < len(steps):
+                t, c0, c1 = steps[i]
+                mates.append(keep.tile([P, c1 - c0], F32, name="mates%d" % i))
+                nc.vector.tensor_copy(mates[i][:], h[t][:].indirect(mate_sb[:, c0 // 16 : c1 // 16]))
+            if i > 0:
+                t, c0, c1 = steps[i - 1]
+                nc.vector.tensor_tensor(mates[i - 1][:], mates[i - 1][:], h[t][:, c0:c1], ALU.min)
+                nc.sync.dma_start(out_rows[t][:, c0:c1], mates[i - 1][:])

@@ -20,13 +20,13 @@ PACK = 4
 HALF = U // 2
 QUARTER = U // 4
 PLANE_ORDER = (2, 0, 1, 3)
+POOL_PIECES = 4
 
 
 def tile_picked_pagemin_none_p_kernel(tc, x_words, x_scales, w1, mem, gn, w2, offs, slot, mate, out):
     nc = tc.nc
     with ExitStack() as ctx:
         keep = ctx.enter_context(tc.tile_pool(name="keep", bufs=1))
-        ring = ctx.enter_context(tc.tile_pool(name="ring", bufs=2))
         psum = ctx.enter_context(tc.psum_pool(name="psum", bufs=1))
 
         offs_sb = keep.tile([P, S // 16], U16, name="offs_sb")
@@ -35,28 +35,22 @@ def tile_picked_pagemin_none_p_kernel(tc, x_words, x_scales, w1, mem, gn, w2, of
         table_words = keep.tile([P, T], I32, name="table_words", align_bytes=64)
         table_scales = keep.tile([P, T], U8, name="table_scales", align_bytes=64)
         gain = keep.tile([P, PACK], F32, name="gain")
-        warm = keep.tile([P, 1], F32, name="warm")
-        warm2 = keep.tile([P, 1], F32, name="warm2")
-        w1_raw = [keep.tile([P, PACK, H // 2], F32, name="w1_raw%d" % c) for c in range(2)]
-        w2_raw = keep.tile([P, PACK, N], F32, name="w2_raw")
-        page = [keep.tile([P, U], F32, name="page%d" % t) for t in range(PACK)]
+        w1_raw = keep.tile([P, PACK, H], F32, name="w1_raw")
+        w2_raw = keep.tile([P, PACK, N], F32, name="w2_raw", align_bytes=64)
+        page = [keep.tile([P, U], F32, name="page%d" % t, align_bytes=64) for t in range(PACK)]
 
         nc.vector.memset(table_scales[:].bitcast(I32), 0)
-        nc.vector.memset(warm[:], 0.0)
         nc.sync.dma_start(offs_sb[:], offs)
         for q in range(4):
             nc.scalar.dma_start(table_scales[32 * q : 32 * q + 4, :].bitcast(I32), x_scales[0, 4 * q : 4 * q + 4, :].bitcast(I32))
-        nc.scalar.activation(warm2[:], warm[:], ACT.Sigmoid)
-        w1_rows = w1.rearrange("(p j) c -> p j c", j=PACK)
-        for c in range(2):
-            nc.sync.dma_start(w1_raw[c][:], w1_rows[:, :, c * (H // 2) : (c + 1) * (H // 2)])
+        nc.sync.dma_start(w1_raw[:], w1.rearrange("(p j) c -> p j c", j=PACK))
         nc.sync.dma_start(table_words[:], x_words[0].rearrange("p c r -> p (c r)").bitcast(I32))
         nc.sync.dma_start(slot_sb[:], slot)
-        nc.sync.dma_start(gain[:], gn.rearrange("(p t) o -> p (t o)", t=PACK))
         mem_rows = mem.rearrange("(p t) w -> t p w", t=PACK)
         for t in PLANE_ORDER:
             nc.sync.dma_start(page[t][:], mem_rows[t])
         nc.sync.dma_start(w2_raw[:], w2.rearrange("(p j) c -> p j c", j=PACK))
+        nc.sync.dma_start(gain[:], gn.rearrange("(p t) o -> p (t o)", t=PACK))
         nc.sync.dma_start(mate_sb[:], mate)
 
         x_codes = keep.tile([P, S], U32, name="x_codes", align_bytes=64)
@@ -65,41 +59,41 @@ def tile_picked_pagemin_none_p_kernel(tc, x_words, x_scales, w1, mem, gn, w2, of
 
         w1_bf = keep.tile([P, PACK * H], BF16, name="w1_bf", align_bytes=64)
         w1_view = w1_bf[:].rearrange("p (t m j) -> p m j t", t=PACK, j=PACK)
-        src = [w1_raw[c][:].rearrange("p j (m t) -> p m j t", t=PACK) for c in range(2)]
-        nc.scalar.copy(w1_view[:, 0:64], src[0])
-        nc.vector.tensor_copy(w1_view[:, 64:128], src[1])
+        w1_src = w1_raw[:].rearrange("p j (m t) -> p m j t", t=PACK)
+        nc.scalar.copy(w1_view[:, 0:44], w1_src[:, 0:44])
+        nc.vector.tensor_copy(w1_view[:, 44:128], w1_src[:, 44:128])
         w1_codes = keep.tile([P, H], U32, name="w1_codes", align_bytes=64)
         w1_scales = keep.tile([P, H], U8, name="w1_scales", align_bytes=64)
         nc.vector.quantize_mx(out=w1_codes[:].bitcast(FP8X4), scales=w1_scales[:], in_=w1_bf[:])
         nc.vector.tensor_copy(x_codes[:], table_words[:].bitcast(U32).indirect(offs_sb[:]))
-        y = {}
+
+        new = {}
+        gate = {}
+        parts = {}
+        bank = 0
         for t in PLANE_ORDER:
             cols = slice(t * P, (t + 1) * P)
-            y[t] = psum.tile([P, S], F32, name="y", tag="bank%d" % t)
-            nc.tensor.matmul_mx(out=y[t][:], lhsT=w1_codes[:, cols].bitcast(FP8X4), lhsT_scale=w1_scales[:, cols],
-                                rhs=x_codes[:].bitcast(FP8X4), rhs_scale=x_bytes[:], start=True, stop=True)
+            old = keep.tile([P, S], F32, name="old%d" % t)
+            nc.vector.tensor_copy(old[:], page[t][:].indirect(slot_sb[:]))
+            gate[t] = keep.tile([P, S], F32, name="gate%d" % t)
+            new[t] = keep.tile([P, S], F32, name="diff%d" % t, align_bytes=64)
+            parts[t] = ((0, S // 2), (S // 2, S)) if t == PLANE_ORDER[0] else ((0, S),)
+            for j0, j1 in parts[t]:
+                y = psum.tile([P, j1 - j0], F32, name="y", tag="bank%d" % bank)
+                bank = bank + 1
+                nc.tensor.matmul_mx(out=y[:], lhsT=w1_codes[:, cols].bitcast(FP8X4), lhsT_scale=w1_scales[:, cols],
+                                    rhs=x_codes[:, j0:j1].bitcast(FP8X4), rhs_scale=x_bytes[:, j0:j1], start=True, stop=True)
+                nc.scalar.activation(gate[t][:, j0:j1], y[:], ACT.Sigmoid)
+                nc.scalar.copy(new[t][:, j0:j1], y[:])
+                nc.gpsimd.tensor_tensor(new[t][:, j0:j1], new[t][:, j0:j1], old[:, j0:j1], ALU.subtract)
+                if t != PLANE_ORDER[-1]:
+                    nc.gpsimd.tensor_tensor(new[t][:, j0:j1], new[t][:, j0:j1], gate[t][:, j0:j1], ALU.mult)
 
+        w2_src = w2_raw[:].rearrange("p j (m t) -> p m j t", t=PACK)
+        w2_early = keep.tile([P, 2 * N], BF16, name="w2_early", align_bytes=64)
+        nc.scalar.copy(w2_early[:].rearrange("p (t m j) -> p m j t", t=2, j=PACK), w2_src[:, :, :, 0:2])
         z_bf = keep.tile([P, U * PACK], BF16, name="z_bf", align_bytes=64)
         z_view = z_bf[:].rearrange("p (w t) -> p t w", t=PACK)
-        w2_bf = keep.tile([P, PACK * N], BF16, name="w2_bf", align_bytes=64)
-        w2_view = w2_bf[:].rearrange("p (t m j) -> p m j t", t=PACK, j=PACK)
-        w2_src = w2_raw[:].rearrange("p j (m t) -> p m j t", t=PACK)
-        w2_codes = keep.tile([P, N], U32, name="w2_codes", align_bytes=64)
-        w2_scales = keep.tile([P, N], U8, name="w2_scales", align_bytes=64)
-
-        diffs = {}
-        gates = {}
-
-        def fetch(t):
-            old = ring.tile([P, S], F32, name="old")
-            nc.vector.tensor_copy(old[:], page[t][:].indirect(slot_sb[:]))
-            gates[t] = ring.tile([P, S], F32, name="gate")
-            nc.scalar.activation(gates[t][:], y[t][:], ACT.Sigmoid)
-            if t == PLANE_ORDER[-1]:
-                diffs[t] = keep.tile([P, S], F32, name="last_diff", tag="page%d" % PLANE_ORDER[0])
-            else:
-                diffs[t] = ring.tile([P, S], F32, name="diff")
-            nc.vector.tensor_tensor(diffs[t][:], y[t][:], old[:], ALU.subtract)
 
         def scale_plane(engine_is_vector, t, c0, c1):
             if engine_is_vector:
@@ -107,18 +101,20 @@ def tile_picked_pagemin_none_p_kernel(tc, x_words, x_scales, w1, mem, gn, w2, of
             else:
                 nc.scalar.activation(z_view[:, t, c0:c1], page[t][:, c0:c1], ACT.Copy, scale=gain[:, t : t + 1])
 
-        fetch(PLANE_ORDER[0])
-        for i, t in enumerate(PLANE_ORDER):
-            if i + 1 < PACK:
-                fetch(PLANE_ORDER[i + 1])
-            nc.vector.tensor_tensor(page[t][:].indirect(slot_sb[:]), diffs[t][:], gates[t][:], ALU.mult)
-            if i == 2:
-                nc.scalar.copy(w2_view[:, :, :, 0:2], w2_src[:, :, :, 0:2])
-                nc.vector.quantize_mx(out=w2_codes[:, 0 : 2 * P].bitcast(FP8X4), scales=w2_scales[:, 0 : 2 * P], in_=w2_bf[:, 0 : 2 * N])
-            if i + 1 < PACK:
-                scale_plane(False, t, 0, U)
-
         last = PLANE_ORDER[-1]
+        for t in PLANE_ORDER[:-1]:
+            for j0, j1 in parts[t]:
+                nc.vector.tensor_copy(page[t][:].indirect(slot_sb[:, j0 // 16 : j1 // 16]), new[t][:, j0:j1])
+            scale_plane(False, t, 0, U)
+            if t == PLANE_ORDER[0]:
+                last_new = keep.tile([P, S], F32, name="last_new", tag="page%d" % t, align_bytes=64)
+                nc.gpsimd.tensor_tensor(last_new[:], new[last][:], gate[last][:], ALU.mult)
+        w2_codes = [keep.tile([P, 2 * P], U32, name="w2_codes0", tag="diff%d" % PLANE_ORDER[2], align_bytes=64),
+                    keep.tile([P, 2 * P], U32, name="w2_codes1", align_bytes=64)]
+        w2_scales = keep.tile([P, N], U8, name="w2_scales", align_bytes=64)
+        nc.vector.quantize_mx(out=w2_codes[0][:].bitcast(FP8X4), scales=w2_scales[:, 0 : 2 * P], in_=w2_early[:])
+        nc.vector.tensor_copy(page[last][:].indirect(slot_sb[:]), last_new[:])
+
         z_codes = keep.tile([P, U], U32, name="z_codes", align_bytes=64)
         z_scales = keep.tile([P, U], U8, name="z_scales", align_bytes=64)
         scale_plane(False, last, HALF, HALF + QUARTER)
@@ -127,36 +123,40 @@ def tile_picked_pagemin_none_p_kernel(tc, x_words, x_scales, w1, mem, gn, w2, of
         pieces = ((HALF, HALF + QUARTER), (0, HALF), (HALF + QUARTER, U))
         for c0, c1 in pieces:
             nc.vector.quantize_mx(out=z_codes[:, c0:c1].bitcast(FP8X4), scales=z_scales[:, c0:c1], in_=z_bf[:, PACK * c0 : PACK * c1])
-        nc.vector.tensor_copy(w2_view[:, :, :, 2:4], w2_src[:, :, :, 2:4])
+        w2_late = keep.tile([P, 2 * N], BF16, name="w2_late", tag="page%d" % PLANE_ORDER[0], align_bytes=64)
+        nc.vector.tensor_copy(w2_late[:].rearrange("p (t m j) -> p m j t", t=2, j=PACK), w2_src[:, :, :, 2:4])
+        nc.vector.quantize_mx(out=w2_codes[1][:].bitcast(FP8X4), scales=w2_scales[:, 2 * P : 4 * P], in_=w2_late[:])
 
         out_rows = out.rearrange("(p t) w -> t p w", t=PACK)
         h = [keep.tile([P, U], F32, name="h%d" % t) for t in range(PACK)]
-        bank = [4]
-
-        def product(t, c0, c1):
+        products = [(0, c0, c1) for c0, c1 in pieces] + [(t, c0, c0 + HALF) for t in range(1, PACK) for c0 in (0, HALF)]
+        acc = {}
+        for i, (t, c0, c1) in enumerate(products):
             cols = slice(t * P, (t + 1) * P)
-            acc = psum.tile([P, c1 - c0], F32, name="acc", tag="bank%d" % (bank[0] % 8))
-            bank[0] = bank[0] + 1
-            nc.tensor.matmul_mx(out=acc[:], lhsT=w2_codes[:, cols].bitcast(FP8X4), lhsT_scale=w2_scales[:, cols],
+            acc[t, c0] = psum.tile([P, c1 - c0], F32, name="acc", tag="bank%d" % ((i + bank) % 8))
+            nc.tensor.matmul_mx(out=acc[t, c0][:], lhsT=w2_codes[t // 2][:, t % 2 * P : (t % 2 + 1) * P].bitcast(FP8X4), lhsT_scale=w2_scales[:, cols],
                                 rhs=z_codes[:, c0:c1].bitcast(FP8X4), rhs_scale=z_scales[:, c0:c1], start=True, stop=True)
-            nc.scalar.copy(h[t][:, c0:c1], acc[:])
-
-        for c0, c1 in pieces:
-            product(0, c0, c1)
-        nc.vector.quantize_mx(out=w2_codes[:, 2 * P : 4 * P].bitcast(FP8X4), scales=w2_scales[:, 2 * P : 4 * P], in_=w2_bf[:, 2 * N : 4 * N])
-        for t in range(1, PACK):
-            for c0 in (0, HALF):
-                product(t, c0, c0 + HALF)
+            nc.scalar.copy(h[t][:, c0:c1], acc[t, c0][:])
 
         steps = [(t, c0, c0 + HALF) for t in range(PACK) for c0 in (0, HALF)][:-1]
         steps = steps + [(PACK - 1, HALF, HALF + QUARTER), (PACK - 1, HALF + QUARTER, U)]
         mates = []
+        excess = []
         for i in range(len(steps) + 1):
             if i < len(steps):
                 t, c0, c1 = steps[i]
                 mates.append(keep.tile([P, c1 - c0], F32, name="mates%d" % i))
                 nc.vector.tensor_copy(mates[i][:], h[t][:].indirect(mate_sb[:, c0 // 16 : c1 // 16]))
+                if i < POOL_PIECES:
+                    excess.append(keep.tile([P, c1 - c0], F32, name="excess", bufs=2))
+                    nc.gpsimd.tensor_tensor(excess[i][:], h[t][:, c0:c1], mates[i][:], ALU.subtract)
+                    nc.scalar.activation(excess[i][:], excess[i][:], ACT.Relu)
             if i > 0:
                 t, c0, c1 = steps[i - 1]
-                nc.vector.tensor_tensor(mates[i - 1][:], mates[i - 1][:], h[t][:, c0:c1], ALU.min)
-                nc.sync.dma_start(out_rows[t][:, c0:c1], mates[i - 1][:])
+                if i - 1 < POOL_PIECES:
+                    nc.gpsimd.tensor_tensor(mates[i - 1][:], h[t][:, c0:c1], excess[i - 1][:], ALU.subtract)
+                else:
+                    b0 = c0 // HALF * HALF
+                    nc.vector.tensor_tensor(mates[i - 1][:], acc[t, b0][:, c0 - b0 : c1 - b0], mates[i - 1][:], ALU.min)
+                queue = nc.scalar if i - 1 < POOL_PIECES else nc.sync
+                queue.dma_start(out_rows[t][:, c0:c1], mates[i - 1][:])

@@ -21,6 +21,7 @@ HALF = U // 2
 QUARTER = U // 4
 PLANE_ORDER = (2, 0, 1, 3)
 POOL_PIECES = 4
+POOL_LAST = 384
 
 
 def tile_picked_pagemin_none_p_kernel(tc, x_words, x_scales, w1, mem, gn, w2, offs, slot, mate, out):
@@ -41,11 +42,11 @@ def tile_picked_pagemin_none_p_kernel(tc, x_words, x_scales, w1, mem, gn, w2, of
 
         nc.vector.memset(table_scales[:].bitcast(I32), 0)
         nc.sync.dma_start(offs_sb[:], offs)
-        for q in range(4):
-            nc.scalar.dma_start(table_scales[32 * q : 32 * q + 4, :].bitcast(I32), x_scales[0, 4 * q : 4 * q + 4, :].bitcast(I32))
-        nc.sync.dma_start(w1_raw[:], w1.rearrange("(p j) c -> p j c", j=PACK))
-        nc.sync.dma_start(table_words[:], x_words[0].rearrange("p c r -> p (c r)").bitcast(I32))
         nc.sync.dma_start(slot_sb[:], slot)
+        nc.sync.dma_start(w1_raw[:], w1.rearrange("(p j) c -> p j c", j=PACK))
+        for q in range(4):
+            nc.sync.dma_start(table_scales[32 * q : 32 * q + 4, :].bitcast(I32), x_scales[0, 4 * q : 4 * q + 4, :].bitcast(I32))
+        nc.sync.dma_start(table_words[:], x_words[0].rearrange("p c r -> p (c r)").bitcast(I32))
         mem_rows = mem.rearrange("(p t) w -> t p w", t=PACK)
         for t in PLANE_ORDER:
             nc.sync.dma_start(page[t][:], mem_rows[t])
@@ -55,17 +56,18 @@ def tile_picked_pagemin_none_p_kernel(tc, x_words, x_scales, w1, mem, gn, w2, of
 
         x_codes = keep.tile([P, S], U32, name="x_codes", align_bytes=64)
         x_bytes = keep.tile([P, S], U8, name="x_bytes", align_bytes=64)
-        nc.vector.tensor_copy(x_bytes[:], table_scales[:].indirect(offs_sb[:]))
 
         w1_bf = keep.tile([P, PACK * H], BF16, name="w1_bf", align_bytes=64)
         w1_view = w1_bf[:].rearrange("p (t m j) -> p m j t", t=PACK, j=PACK)
         w1_src = w1_raw[:].rearrange("p j (m t) -> p m j t", t=PACK)
-        nc.scalar.copy(w1_view[:, 0:44], w1_src[:, 0:44])
-        nc.vector.tensor_copy(w1_view[:, 44:128], w1_src[:, 44:128])
+        nc.scalar.copy(w1_view[:, 0:56], w1_src[:, 0:56])
+        nc.vector.tensor_copy(w1_view[:, 56:128], w1_src[:, 56:128])
+        nc.vector.tensor_copy(x_bytes[:], table_scales[:].indirect(offs_sb[:]))
         w1_codes = keep.tile([P, H], U32, name="w1_codes", align_bytes=64)
         w1_scales = keep.tile([P, H], U8, name="w1_scales", align_bytes=64)
         nc.vector.quantize_mx(out=w1_codes[:].bitcast(FP8X4), scales=w1_scales[:], in_=w1_bf[:])
-        nc.vector.tensor_copy(x_codes[:], table_words[:].bitcast(U32).indirect(offs_sb[:]))
+        for j0 in (0, S // 2):
+            nc.vector.tensor_copy(x_codes[:, j0 : j0 + S // 2], table_words[:].bitcast(U32).indirect(offs_sb[:, j0 // 16 : (j0 + S // 2) // 16]))
 
         new = {}
         gate = {}
@@ -74,18 +76,21 @@ def tile_picked_pagemin_none_p_kernel(tc, x_words, x_scales, w1, mem, gn, w2, of
         for t in PLANE_ORDER:
             cols = slice(t * P, (t + 1) * P)
             old = keep.tile([P, S], F32, name="old%d" % t)
-            nc.vector.tensor_copy(old[:], page[t][:].indirect(slot_sb[:]))
-            gate[t] = keep.tile([P, S], F32, name="gate%d" % t)
+            gate[t] = keep.tile([P, S], F32, name="gate%d" % t, align_bytes=64)
             new[t] = keep.tile([P, S], F32, name="diff%d" % t, align_bytes=64)
             parts[t] = ((0, S // 2), (S // 2, S)) if t == PLANE_ORDER[0] else ((0, S),)
             for j0, j1 in parts[t]:
+                nc.vector.tensor_copy(old[:, j0:j1], page[t][:].indirect(slot_sb[:, j0 // 16 : j1 // 16]))
                 y = psum.tile([P, j1 - j0], F32, name="y", tag="bank%d" % bank)
                 bank = bank + 1
                 nc.tensor.matmul_mx(out=y[:], lhsT=w1_codes[:, cols].bitcast(FP8X4), lhsT_scale=w1_scales[:, cols],
                                     rhs=x_codes[:, j0:j1].bitcast(FP8X4), rhs_scale=x_bytes[:, j0:j1], start=True, stop=True)
                 nc.scalar.activation(gate[t][:, j0:j1], y[:], ACT.Sigmoid)
-                nc.scalar.copy(new[t][:, j0:j1], y[:])
-                nc.gpsimd.tensor_tensor(new[t][:, j0:j1], new[t][:, j0:j1], old[:, j0:j1], ALU.subtract)
+                if t == PLANE_ORDER[1]:
+                    nc.vector.tensor_tensor(new[t][:, j0:j1], y[:], old[:, j0:j1], ALU.subtract)
+                else:
+                    nc.scalar.copy(new[t][:, j0:j1], y[:])
+                    nc.gpsimd.tensor_tensor(new[t][:, j0:j1], new[t][:, j0:j1], old[:, j0:j1], ALU.subtract)
                 if t != PLANE_ORDER[-1]:
                     nc.gpsimd.tensor_tensor(new[t][:, j0:j1], new[t][:, j0:j1], gate[t][:, j0:j1], ALU.mult)
 
@@ -109,22 +114,21 @@ def tile_picked_pagemin_none_p_kernel(tc, x_words, x_scales, w1, mem, gn, w2, of
             if t == PLANE_ORDER[0]:
                 last_new = keep.tile([P, S], F32, name="last_new", tag="page%d" % t, align_bytes=64)
                 nc.gpsimd.tensor_tensor(last_new[:], new[last][:], gate[last][:], ALU.mult)
-        w2_codes = [keep.tile([P, 2 * P], U32, name="w2_codes0", tag="diff%d" % PLANE_ORDER[2], align_bytes=64),
-                    keep.tile([P, 2 * P], U32, name="w2_codes1", align_bytes=64)]
+        w2_codes = [keep.tile([P, 2 * P], U32, name="w2_codes0", tag="diff%d" % PLANE_ORDER[2], align_bytes=64)]
         w2_scales = keep.tile([P, N], U8, name="w2_scales", align_bytes=64)
         nc.vector.quantize_mx(out=w2_codes[0][:].bitcast(FP8X4), scales=w2_scales[:, 0 : 2 * P], in_=w2_early[:])
+        w2_late = keep.tile([P, 2 * N], BF16, name="w2_late", tag="gate%d" % last, align_bytes=64)
+        nc.gpsimd.tensor_scalar(w2_late[:].rearrange("p (t m j) -> p t m j", t=2, j=PACK), w2_raw[:].rearrange("p j (m t) -> p t m j", t=PACK)[:, 2:4], 1.0, 0.0, ALU.mult, ALU.add)
         nc.vector.tensor_copy(page[last][:].indirect(slot_sb[:]), last_new[:])
 
         z_codes = keep.tile([P, U], U32, name="z_codes", align_bytes=64)
         z_scales = keep.tile([P, U], U8, name="z_scales", align_bytes=64)
-        scale_plane(False, last, HALF, HALF + QUARTER)
-        scale_plane(True, last, 0, HALF)
-        scale_plane(False, last, HALF + QUARTER, U)
-        pieces = ((HALF, HALF + QUARTER), (0, HALF), (HALF + QUARTER, U))
+        pieces = [(c0, c0 + QUARTER) for c0 in range(0, U, QUARTER)]
+        for c0, c1 in pieces:
+            scale_plane(c0 < HALF, last, c0, c1)
         for c0, c1 in pieces:
             nc.vector.quantize_mx(out=z_codes[:, c0:c1].bitcast(FP8X4), scales=z_scales[:, c0:c1], in_=z_bf[:, PACK * c0 : PACK * c1])
-        w2_late = keep.tile([P, 2 * N], BF16, name="w2_late", tag="page%d" % PLANE_ORDER[0], align_bytes=64)
-        nc.vector.tensor_copy(w2_late[:].rearrange("p (t m j) -> p m j t", t=2, j=PACK), w2_src[:, :, :, 2:4])
+        w2_codes.append(keep.tile([P, 2 * P], U32, name="w2_codes1", tag="page%d" % last, align_bytes=64))
         nc.vector.quantize_mx(out=w2_codes[1][:].bitcast(FP8X4), scales=w2_scales[:, 2 * P : 4 * P], in_=w2_late[:])
 
         out_rows = out.rearrange("(p t) w -> t p w", t=PACK)
@@ -136,7 +140,10 @@ def tile_picked_pagemin_none_p_kernel(tc, x_words, x_scales, w1, mem, gn, w2, of
             acc[t, c0] = psum.tile([P, c1 - c0], F32, name="acc", tag="bank%d" % ((i + bank) % 8))
             nc.tensor.matmul_mx(out=acc[t, c0][:], lhsT=w2_codes[t // 2][:, t % 2 * P : (t % 2 + 1) * P].bitcast(FP8X4), lhsT_scale=w2_scales[:, cols],
                                 rhs=z_codes[:, c0:c1].bitcast(FP8X4), rhs_scale=z_scales[:, c0:c1], start=True, stop=True)
-            nc.scalar.copy(h[t][:, c0:c1], acc[t, c0][:])
+            if i == 2:
+                nc.vector.tensor_copy(h[t][:, c0:c1], acc[t, c0][:])
+            else:
+                nc.scalar.copy(h[t][:, c0:c1], acc[t, c0][:])
 
         steps = [(t, c0, c0 + HALF) for t in range(PACK) for c0 in (0, HALF)][:-1]
         steps = steps + [(PACK - 1, HALF, HALF + QUARTER), (PACK - 1, HALF + QUARTER, U)]
@@ -145,18 +152,22 @@ def tile_picked_pagemin_none_p_kernel(tc, x_words, x_scales, w1, mem, gn, w2, of
         for i in range(len(steps) + 1):
             if i < len(steps):
                 t, c0, c1 = steps[i]
-                mates.append(keep.tile([P, c1 - c0], F32, name="mates%d" % i))
+                mates.append(keep.tile([P, c1 - c0], F32, name="mates", tag="mates%d" % i))
                 nc.vector.tensor_copy(mates[i][:], h[t][:].indirect(mate_sb[:, c0 // 16 : c1 // 16]))
                 if i < POOL_PIECES:
-                    excess.append(keep.tile([P, c1 - c0], F32, name="excess", bufs=2))
-                    nc.gpsimd.tensor_tensor(excess[i][:], h[t][:, c0:c1], mates[i][:], ALU.subtract)
+                    width = c1 - c0 if i + 1 < POOL_PIECES else POOL_LAST
+                    excess.append(keep.tile([P, width], F32, name="excess", bufs=2))
+                    nc.gpsimd.tensor_tensor(excess[i][:], h[t][:, c0 : c0 + width], mates[i][:, 0:width], ALU.subtract)
                     nc.scalar.activation(excess[i][:], excess[i][:], ACT.Relu)
             if i > 0:
                 t, c0, c1 = steps[i - 1]
+                least = keep.tile([P, c1 - c0], F32, name="least%d" % i)
+                width = 0
                 if i - 1 < POOL_PIECES:
-                    nc.gpsimd.tensor_tensor(mates[i - 1][:], h[t][:, c0:c1], excess[i - 1][:], ALU.subtract)
-                else:
+                    width = c1 - c0 if i < POOL_PIECES else POOL_LAST
+                    nc.gpsimd.tensor_tensor(least[:, 0:width], h[t][:, c0 : c0 + width], excess[i - 1][:], ALU.subtract)
+                    nc.scalar.dma_start(out_rows[t][:, c0 : c0 + width], least[:, 0:width])
+                if width < c1 - c0:
                     b0 = c0 // HALF * HALF
-                    nc.vector.tensor_tensor(mates[i - 1][:], acc[t, b0][:, c0 - b0 : c1 - b0], mates[i - 1][:], ALU.min)
-                queue = nc.scalar if i - 1 < POOL_PIECES else nc.sync
-                queue.dma_start(out_rows[t][:, c0:c1], mates[i - 1][:])
+                    nc.vector.tensor_tensor(least[:, width:], acc[t, b0][:, c0 + width - b0 : c1 - b0], mates[i - 1][:, width:], ALU.min)
+                    nc.sync.dma_start(out_rows[t][:, c0 + width : c1], least[:, width:])

@@ -115,9 +115,10 @@ def tile_picked_pagemin_none_p_kernel(tc, x_words, x_scales, w1, mem, gn, w2, of
                 last_new = keep.tile([P, S], F32, name="last_new", tag="page%d" % t, align_bytes=64)
                 nc.gpsimd.tensor_tensor(last_new[:], new[last][:], gate[last][:], ALU.mult)
         w2_codes = [keep.tile([P, 2 * P], U32, name="w2_codes0", tag="diff%d" % PLANE_ORDER[2], align_bytes=64)]
-        w2_scales = keep.tile([P, N], U8, name="w2_scales", align_bytes=64)
-        nc.vector.quantize_mx(out=w2_codes[0][:].bitcast(FP8X4), scales=w2_scales[:, 0 : 2 * P], in_=w2_early[:])
-        w2_late = keep.tile([P, 2 * N], BF16, name="w2_late", tag="gate%d" % last, align_bytes=64)
+        w2_scales = [keep.tile([P, 2 * P], U8, name="w2_scales0", tag="gate%d" % last, align_bytes=64),
+                     keep.tile([P, 2 * P], U8, name="w2_scales1", align_bytes=64)]
+        nc.vector.quantize_mx(out=w2_codes[0][:].bitcast(FP8X4), scales=w2_scales[0][:], in_=w2_early[:])
+        w2_late = keep.tile([P, 2 * N], BF16, name="w2_late", tag="w2_early", align_bytes=64)
         nc.gpsimd.tensor_scalar(w2_late[:].rearrange("p (t m j) -> p t m j", t=2, j=PACK), w2_raw[:].rearrange("p j (m t) -> p t m j", t=PACK)[:, 2:4], 1.0, 0.0, ALU.mult, ALU.add)
         nc.vector.tensor_copy(page[last][:].indirect(slot_sb[:]), last_new[:])
 
@@ -129,7 +130,7 @@ def tile_picked_pagemin_none_p_kernel(tc, x_words, x_scales, w1, mem, gn, w2, of
         for c0, c1 in pieces:
             nc.vector.quantize_mx(out=z_codes[:, c0:c1].bitcast(FP8X4), scales=z_scales[:, c0:c1], in_=z_bf[:, PACK * c0 : PACK * c1])
         w2_codes.append(keep.tile([P, 2 * P], U32, name="w2_codes1", tag="page%d" % last, align_bytes=64))
-        nc.vector.quantize_mx(out=w2_codes[1][:].bitcast(FP8X4), scales=w2_scales[:, 2 * P : 4 * P], in_=w2_late[:])
+        nc.vector.quantize_mx(out=w2_codes[1][:].bitcast(FP8X4), scales=w2_scales[1][:], in_=w2_late[:])
 
         out_rows = out.rearrange("(p t) w -> t p w", t=PACK)
         h = [keep.tile([P, U], F32, name="h%d" % t) for t in range(PACK)]
@@ -138,7 +139,7 @@ def tile_picked_pagemin_none_p_kernel(tc, x_words, x_scales, w1, mem, gn, w2, of
         for i, (t, c0, c1) in enumerate(products):
             cols = slice(t * P, (t + 1) * P)
             acc[t, c0] = psum.tile([P, c1 - c0], F32, name="acc", tag="bank%d" % ((i + bank) % 8))
-            nc.tensor.matmul_mx(out=acc[t, c0][:], lhsT=w2_codes[t // 2][:, t % 2 * P : (t % 2 + 1) * P].bitcast(FP8X4), lhsT_scale=w2_scales[:, cols],
+            nc.tensor.matmul_mx(out=acc[t, c0][:], lhsT=w2_codes[t // 2][:, t % 2 * P : (t % 2 + 1) * P].bitcast(FP8X4), lhsT_scale=w2_scales[t // 2][:, t % 2 * P : (t % 2 + 1) * P],
                                 rhs=z_codes[:, c0:c1].bitcast(FP8X4), rhs_scale=z_scales[:, c0:c1], start=True, stop=True)
             if i == 2:
                 nc.vector.tensor_copy(h[t][:, c0:c1], acc[t, c0][:])

from contextlib import ExitStack

import concourse.mybir as mybir

K, T, S, N, H, U = 512, 2048, 512, 512, 512, 1024
FLOPS = 2 * K * H * S + 2 * H * N * U

F32 = mybir.dt.float32
BF16 = mybir.dt.bfloat16
I32 = mybir.dt.int32
U32 = mybir.dt.uint32
U16 = mybir.dt.uint16
U8 = mybir.dt.uint8
FP8X4 = mybir.dt.float8_e4m3fn_x4
ALU = mybir.AluOpType
ACT = mybir.ActivationFunctionType

P = 128
PACK = 4
HALF = U // 2
QUARTER = U // 4
PLANE_ORDER = (2, 0, 1, 3)
POOL_PIECES = 4
POOL_LAST = 384


def tile_picked_pagemin_none_p_kernel(tc, x_words, x_scales, w1, mem, gn, w2, offs, slot, mate, out):
    nc = tc.nc
    with ExitStack() as ctx:
        keep = ctx.enter_context(tc.tile_pool(name="keep", bufs=1))
        psum = ctx.enter_context(tc.psum_pool(name="psum", bufs=1))

        offs_sb = keep.tile([P, S // 16], U16, name="offs_sb")
        slot_sb = keep.tile([P, S // 16], U16, name="slot_sb")
        mate_sb = keep.tile([P, U // 16], U16, name="mate_sb")
        table_words = keep.tile([P, T], I32, name="table_words", align_bytes=64)
        table_scales = keep.tile([P, T], U8, name="table_scales", align_bytes=64)
        gain = keep.tile([P, PACK], F32, name="gain")
        w1_raw = keep.tile([P, PACK, H], F32, name="w1_raw")
        w2_raw = keep.tile([P, PACK, N], F32, name="w2_raw", align_bytes=64)
        page = [keep.tile([P, U], F32, name="page%d" % t, align_bytes=64) for t in range(PACK)]

        nc.vector.memset(table_scales[:].bitcast(I32), 0)
        nc.sync.dma_start(offs_sb[:], offs)
        nc.sync.dma_start(slot_sb[:], slot)
        nc.sync.dma_start(w1_raw[:], w1.rearrange("(p j) c -> p j c", j=PACK))
        for q in range(4):
            nc.sync.dma_start(table_scales[32 * q : 32 * q + 4, :].bitcast(I32), x_scales[0, 4 * q : 4 * q + 4, :].bitcast(I32))
        nc.sync.dma_start(table_words[:], x_words[0].rearrange("p c r -> p (c r)").bitcast(I32))
        mem_rows = mem.rearrange("(p t) w -> t p w", t=PACK)
        for t in PLANE_ORDER:
            nc.sync.dma_start(page[t][:], mem_rows[t])
        nc.sync.dma_start(w2_raw[:], w2.rearrange("(p j) c -> p j c", j=PACK))
        nc.sync.dma_start(gain[:], gn.rearrange("(p t) o -> p (t o)", t=PACK))
        nc.sync.dma_start(mate_sb[:], mate)

        x_codes = keep.tile([P, S], U32, name="x_codes", align_bytes=64)
        x_bytes = keep.tile([P, S], U8, name="x_bytes", align_bytes=64)

        w1_bf = keep.tile([P, PACK * H], BF16, name="w1_bf", align_bytes=64)
        w1_view = w1_bf[:].rearrange("p (t m j) -> p m j t", t=PACK, j=PACK)
        w1_src = w1_raw[:].rearrange("p j (m t) -> p m j t", t=PACK)
        nc.scalar.copy(w1_view[:, 0:56], w1_src[:, 0:56])
        nc.vector.tensor_copy(w1_view[:, 56:128], w1_src[:, 56:128])
        nc.vector.tensor_copy(x_bytes[:], table_scales[:].indirect(offs_sb[:]))
        w1_codes = keep.tile([P, H], U32, name="w1_codes", align_bytes=64)
        w1_scales = keep.tile([P, H], U8, name="w1_scales", align_bytes=64)
        nc.vector.quantize_mx(out=w1_codes[:].bitcast(FP8X4), scales=w1_scales[:], in_=w1_bf[:])
        for j0 in (0, S // 2):
            nc.vector.tensor_copy(x_codes[:, j0 : j0 + S // 2], table_words[:].bitcast(U32).indirect(offs_sb[:, j0 // 16 : (j0 + S // 2) // 16]))

        new = {}
        gate = {}
        parts = {}
        bank = 0
        for t in PLANE_ORDER:
            cols = slice(t * P, (t + 1) * P)
            old = keep.tile([P, S], F32, name="old%d" % t)
            gate[t] = keep.tile([P, S], F32, name="gate%d" % t, align_bytes=64)
            new[t] = keep.tile([P, S], F32, name="diff%d" % t, align_bytes=64)
            parts[t] = ((0, S // 2), (S // 2, S)) if t == PLANE_ORDER[0] else ((0, S),)
            for j0, j1 in parts[t]:
                nc.vector.tensor_copy(old[:, j0:j1], page[t][:].indirect(slot_sb[:, j0 // 16 : j1 // 16]))
                y = psum.tile([P, j1 - j0], F32, name="y", tag="bank%d" % bank)
                bank = bank + 1
                nc.tensor.matmul_mx(out=y[:], lhsT=w1_codes[:, cols].bitcast(FP8X4), lhsT_scale=w1_scales[:, cols],
                                    rhs=x_codes[:, j0:j1].bitcast(FP8X4), rhs_scale=x_bytes[:, j0:j1], start=True, stop=True)
                nc.scalar.activation(gate[t][:, j0:j1], y[:], ACT.Sigmoid)
                if t == PLANE_ORDER[1]:
                    nc.vector.tensor_tensor(new[t][:, j0:j1], y[:], old[:, j0:j1], ALU.subtract)
                else:
                    nc.scalar.copy(new[t][:, j0:j1], y[:])
                    nc.gpsimd.tensor_tensor(new[t][:, j0:j1], new[t][:, j0:j1], old[:, j0:j1], ALU.subtract)
                if t != PLANE_ORDER[-1]:
                    nc.gpsimd.tensor_tensor(new[t][:, j0:j1], new[t][:, j0:j1], gate[t][:, j0:j1], ALU.mult)

        w2_src = w2_raw[:].rearrange("p j (m t) -> p m j t", t=PACK)
        w2_early = keep.tile([P, 2 * N], BF16, name="w2_early", align_bytes=64)
        nc.scalar.copy(w2_early[:].rearrange("p (t m j) -> p m j t", t=2, j=PACK), w2_src[:, :, :, 0:2])
        z_bf = keep.tile([P, U * PACK], BF16, name="z_bf", align_bytes=64)
        z_view = z_bf[:].rearrange("p (w t) -> p t w", t=PACK)

        def scale_plane(engine_is_vector, t, c0, c1):
            if engine_is_vector:
                nc.vector.tensor_scalar(z_view[:, t, c0:c1], page[t][:, c0:c1], gain[:, t : t + 1], None, ALU.mult)
            else:
                nc.scalar.activation(z_view[:, t, c0:c1], page[t][:, c0:c1], ACT.Copy, scale=gain[:, t : t + 1])

        last = PLANE_ORDER[-1]
        for t in PLANE_ORDER[:-1]:
            for j0, j1 in parts[t]:
                nc.vector.tensor_copy(page[t][:].indirect(slot_sb[:, j0 // 16 : j1 // 16]), new[t][:, j0:j1])
            scale_plane(False, t, 0, U)
            if t == PLANE_ORDER[0]:
                last_new = keep.tile([P, S], F32, name="last_new", tag="page%d" % t, align_bytes=64)
                nc.gpsimd.tensor_tensor(last_new[:], new[last][:], gate[last][:], ALU.mult)
        w2_codes = [keep.tile([P, 2 * P], U32, name="w2_codes0", tag="diff%d" % PLANE_ORDER[2], align_bytes=64)]
        w2_scales = [keep.tile([P, 2 * P], U8, name="w2_scales0", tag="gate%d" % last, align_bytes=64),
                     keep.tile([P, 2 * P], U8, name="w2_scales1", align_bytes=64)]
        nc.vector.quantize_mx(out=w2_codes[0][:].bitcast(FP8X4), scales=w2_scales[0][:], in_=w2_early[:])
        w2_late = keep.tile([P, 2 * N], BF16, name="w2_late", tag="w2_early", align_bytes=64)
        nc.gpsimd.tensor_scalar(w2_late[:].rearrange("p (t m j) -> p t m j", t=2, j=PACK), w2_raw[:].rearrange("p j (m t) -> p t m j", t=PACK)[:, 2:4], 1.0, 0.0, ALU.mult, ALU.add)
        nc.vector.tensor_copy(page[last][:].indirect(slot_sb[:]), last_new[:])

        z_codes = keep.tile([P, U], U32, name="z_codes", align_bytes=64)
        z_scales = keep.tile([P, U], U8, name="z_scales", align_bytes=64)
        pieces = [(c0, c0 + QUARTER) for c0 in range(0, U, QUARTER)]
        for c0, c1 in pieces:
            scale_plane(c0 < HALF, last, c0, c1)
        for c0, c1 in pieces:
            nc.vector.quantize_mx(out=z_codes[:, c0:c1].bitcast(FP8X4), scales=z_scales[:, c0:c1], in_=z_bf[:, PACK * c0 : PACK * c1])
        w2_codes.append(keep.tile([P, 2 * P], U32, name="w2_codes1", tag="page%d" % last, align_bytes=64))
        nc.vector.quantize_mx(out=w2_codes[1][:].bitcast(FP8X4), scales=w2_scales[1][:], in_=w2_late[:])

        out_rows = out.rearrange("(p t) w -> t p w", t=PACK)
        h = [keep.tile([P, U], F32, name="h%d" % t) for t in range(PACK)]
        products = [(0, c0, c1) for c0, c1 in pieces] + [(t, c0, c0 + HALF) for t in range(1, PACK) for c0 in (0, HALF)]
        acc = {}
        for i, (t, c0, c1) in enumerate(products):
            cols = slice(t * P, (t + 1) * P)
            acc[t, c0] = psum.tile([P, c1 - c0], F32, name="acc", tag="bank%d" % ((i + bank) % 8))
            nc.tensor.matmul_mx(out=acc[t, c0][:], lhsT=w2_codes[t // 2][:, t % 2 * P : (t % 2 + 1) * P].bitcast(FP8X4), lhsT_scale=w2_scales[t // 2][:, t % 2 * P : (t % 2 + 1) * P],
                                rhs=z_codes[:, c0:c1].bitcast(FP8X4), rhs_scale=z_scales[:, c0:c1], start=True, stop=True)
            if i == 2:
                nc.vector.tensor_copy(h[t][:, c0:c1], acc[t, c0][:])
            else:
                nc.scalar.copy(h[t][:, c0:c1], acc[t, c0][:])

        steps = [(t, c0, c0 + HALF) for t in range(PACK) for c0 in (0, HALF)][:-1]
        steps = steps + [(PACK - 1, HALF, HALF + QUARTER), (PACK - 1, HALF + QUARTER, U)]
        mates = []
        excess = []
        for i in range(len(steps) + 1):
            if i < len(steps):
                t, c0, c1 = steps[i]
                mates.append(keep.tile([P, c1 - c0], F32, name="mates", tag="mates%d" % i))
                nc.vector.tensor_copy(mates[i][:], h[t][:].indirect(mate_sb[:, c0 // 16 : c1 // 16]))
                if i < POOL_PIECES:
                    width = c1 - c0 if i + 1 < POOL_PIECES else POOL_LAST
                    excess.append(keep.tile([P, width], F32, name="excess", bufs=2))
                    nc.gpsimd.tensor_tensor(excess[i][:], h[t][:, c0 : c0 + width], mates[i][:, 0:width], ALU.subtract)
                    nc.scalar.activation(excess[i][:], excess[i][:], ACT.Relu)
            if i > 0:
                t, c0, c1 = steps[i - 1]
                least = keep.tile([P, c1 - c0], F32, name="least%d" % i)
                width = 0
                if i - 1 < POOL_PIECES:
                    width = c1 - c0 if i < POOL_PIECES else POOL_LAST
                    nc.gpsimd.tensor_tensor(least[:, 0:width], h[t][:, c0 : c0 + width], excess[i - 1][:], ALU.subtract)
                    nc.scalar.dma_start(out_rows[t][:, c0 : c0 + width], least[:, 0:width])
                if width < c1 - c0:
                    b0 = c0 // HALF * HALF
                    nc.vector.tensor_tensor(least[:, width:], acc[t, b0][:, c0 + width - b0 : c1 - b0], mates[i - 1][:, width:], ALU.min)
                    nc.sync.dma_start(out_rows[t][:, c0 + width : c1], least[:, width:])
